import numpy as np, ml_dtypes
CORES = [10,34,74,98]
N = 4
BF = ml_dtypes.bfloat16
def gentries(a):
    return np.ascontiguousarray(a.reshape(8, 16, -1).transpose(0, 2, 1)).reshape(8, -1)
def gtable(e):
    e = np.asarray(e); return np.ascontiguousarray(e.reshape(8, -1, 16).transpose(0, 2, 1)).reshape(128, -1).astype(np.int32)
W, NB, T, CA, LV, LI, LG = 4096, 4096, 6, 4, 8, 2, 2
P, S = NB // 16, W // (NB // 16)
def parts(rng):
    return rng.integers(0, 256, (N, 8, 16, W)), rng.integers(0, 256, (N, 8, 16, P)), rng.integers(0, 16, (N, 8, 16)), rng.integers(0, W, (N, 8, NB)), rng.integers(0, W, (N, 8, NB))
def pack(x, z, w, a, b):
    return {"xt": np.reshape(x, (N, 128, W)).astype(np.float32).astype(BF), "zp": np.reshape(z, (N, 128, P)).astype(np.float32).astype(BF), "wl": np.reshape(w, (N, 128, 1)).astype(np.float32).astype(BF),
            "ba": np.stack([gtable(v) for v in a]), "bb": np.stack([gtable(v) for v in b])}
def setup_inputs(rng):
    x, z, w, a, b = parts(rng)
    return pack(x, z, w, a, np.where(rng.random(b.shape) < 0.125, a, b))
def setup_inputs_corners(rng):
    x, z, w, a, b = parts(rng); pol = 255 * (np.arange(8) & 1)
    good = rng.random((N, 8, W)) < 0.5; good[..., W - 4:W - 1] = False
    far = np.abs(pol[None, :, None, None] - rng.integers(128, 256, x.shape))
    x = np.where(good[:, :, None, :], pol[None, :, None, None], far)
    z = np.broadcast_to(pol[None, :, None, None], z.shape).copy()
    o = np.argsort(rng.random((N, 8, 16)), axis=-1); v = rng.choice(np.array([128, 200]), (N, 8, 16))
    x[..., W - 4] = 128; x[..., W - 3] = np.where(o < LV, v, 60); x[..., W - 2] = np.where(o < LV - 1, v, 60)
    own = np.arange(NB).reshape(P, 16)
    for q in range(N):
        for g in range(8):
            pa, pb = rng.integers(0, W, 8192), rng.integers(0, W, 8192); pc = ((pa * pb >> 5) + pa + 37 * pb) & (W - 1); k = good[q, g]
            yes = np.flatnonzero(~k[pa] & ~k[pb] & k[pc] & (pa != pb)); no = np.flatnonzero((k[pa] | k[pb]) & (pa != pb))
            n = rng.choice(np.array([0, 1, CA - 1, CA, CA + 1, 16]), P); n[P - 1] = CA; n[0] = 16; n[2] = CA + 1
            m = np.argsort(rng.random((P, 16)), axis=1) < n[:, None]
            i = np.where(m, yes[rng.integers(0, len(yes), (P, 16))], no[rng.integers(0, len(no), (P, 16))]); aa, bb = pa[i], pb[i]
            kp = rng.integers(0, 12, P); kp[0] = 9; kp[P - 1] = 9; kp[2] = 9; kp[1] = 2; kp[P - 2] = 3; kp[3] = 0; kp[P - 3] = 1
            s = (kp == 0) | (kp == 2) | (kp == 3); aa[s] = own[s]; bb[s] = own[s]
            e = (W - 1) * rng.integers(0, 2, (P, 16)); aa[kp == 1] = e[kp == 1]; bb[kp == 1] = e[kp == 1]
            aa[kp == 4] = e[kp == 4]; bb[kp == 4] = W - 1 - e[kp == 4]
            slot = rng.integers(0, 16, P)
            for c, col in ((2, W - 3), (3, W - 2)):
                r = np.flatnonzero(kp == c); aa[r, slot[r]] = W - 4; bb[r, slot[r]] = col; z[q, g][:, r] = x[q, g, :, col][:, None]
            a[q, g] = aa.reshape(-1); b[q, g] = bb.reshape(-1)
    b[1] = a[1]
    w[:, 0] = 0; w[:, 1] = 15; w[:, 2] = 0; w[:, 2, 15] = 15; w[:, 3] = 15 * rng.integers(0, 2, (N, 16))
    return pack(x, z, w, a, b)
def setup_inputs_ends(rng):
    kind = rng.integers(0, 4, (N, 8, 1, W)); x = 255 * np.where(kind > 1, rng.integers(0, 2, (N, 8, 16, W)), kind)
    x = np.where((kind == 3) & (rng.random(x.shape) < 0.25), x ^ 1, x)
    hi = np.arange(8) & 1
    x[..., 0] = 255 * (1 - hi)[None, :, None]; x[..., W - 1] = 255 * hi[None, :, None]; x[0, ::2, :, W - 37] = 255
    cc = (((W - 1) * (W - 2) >> 5) + W - 1 + 37 * (W - 2)) & (W - 1)
    x[:, 1::2, :, W - 2] = 255; x[:, 1::2, :, cc] = 255
    zk = rng.integers(0, 3, (N, 8, 1, P)); z = 255 * np.where(zk == 2, rng.integers(0, 2, (N, 8, 16, P)), zk)
    w = 15 * rng.integers(0, 2, (N, 8, 16)); w[:, 1] = 15; w[:, 7] = 15; w[:, 2] = 0
    sh = (N, 8, NB)
    a = np.where(rng.random(sh) < 0.8, (W - 1) * rng.integers(0, 2, sh), rng.integers(0, W, sh))
    b = np.where(rng.random(sh) < 0.8, (W - 1) * rng.integers(0, 2, sh), rng.integers(0, W, sh))
    n = rng.integers(10, 17, (8, P, 1)); n[:, 0] = 16; n[:, P - 1] = 16
    m = (np.argsort(rng.random((8, P, 16)), axis=-1) < n).reshape(8, NB); top = ((W - 1) * hi)[:, None]
    a[0] = np.where(m, top, a[0]); b[0] = np.where(m, W - 1 - top, b[0])
    z[0] = 255 * (np.argsort(rng.random((8, 16, P)), axis=1) < rng.integers(0, 7, (8, 1, P)))
    for q in range(1, N):
        for g in (1, 7):
            for i, va, vb, vz in ((0, 0, W - 1, 255), (P - 1, 0, W - 1, 255), (1, W - 1, 0, 0), (P - 2, W - 1, 0, 0), (2, W - 1, W - 2, 0), (P - 3, W - 1, W - 2, 0)):
                a[q, g, 16 * i:16 * i + 16] = va; b[q, g, 16 * i:16 * i + 16] = vb; z[q, g, :, i] = vz
    return pack(x, z, w, a, b)
def setup_inputs_spread(rng):
    x, z, w, a, b = parts(rng)
    x = (np.exp2(8 * rng.random((N, 8, 1, W))) * rng.random(x.shape)).astype(np.int64)
    z = (np.exp2(8 * rng.random((N, 8, 1, P))) * rng.random(z.shape)).astype(np.int64)
    w = w >> rng.integers(0, 5, w.shape)
    a = (W * rng.random(a.shape) ** rng.integers(1, 5, (N, 8, 1))).astype(np.int64); b = (W * rng.random(b.shape) ** rng.integers(1, 5, (N, 8, 1))).astype(np.int64)
    return pack(x, z, w, np.minimum(a, W - 1), np.minimum(b, W - 1))
def setup_inputs_ties(rng):
    x, z, w, a, b = parts(rng)
    base = rng.integers(0, 256, (N, 8, 16, 6)); base[:, ::2] = rng.choice(np.array([0, 1, 128, 254, 255]), (N, 4, 16, 6))
    x = np.take_along_axis(base, rng.integers(0, 6, (N, 8, 1, W)), 3)
    z = np.where(rng.random((N, 8, 1, P)) < 0.75, np.take_along_axis(base, rng.integers(0, 6, (N, 8, 1, P)), 3), z)
    m = rng.random((N, 8, P, 1)) < 0.25
    a = a.reshape(N, 8, P, 16); b = b.reshape(N, 8, P, 16); b = np.where(rng.random(b.shape) < 0.125, a, b)
    a = np.where(m, a[..., :1], a).reshape(N, 8, NB); b = np.where(m, b[..., :1], b).reshape(N, 8, NB)
    return pack(x, z, w, a, b)
def check_inputs(d):
    bad = []
    for k, lo, hi in (("xt", 0, 255), ("zp", 0, 255), ("wl", 0, 15), ("ba", 0, W - 1), ("bb", 0, W - 1)):
        v = np.asarray(d[k]).astype(np.float64)
        if not np.all((v >= lo) & (v <= hi) & (v == np.floor(v))): bad.append("range of " + k)
    return bad
def reference(xt, zp, wl, ba, bb):
    X = xt.astype(np.float32).astype(np.int32).reshape(N, 8, 16, W); z = zp.astype(np.float32).astype(np.int32).reshape(N, 8, 16, P)
    w = wl.astype(np.float32).astype(np.int32).reshape(N, 8, 16, 1)
    L = [np.stack([gentries(v) for v in m]).astype(np.int32) for m in (ba, bb)]
    I = np.zeros((N, 8, NB), np.int32); G = np.zeros((N, 8, NB), np.int32); rej = [0] * N
    def before(m):
        m = m.astype(np.int32).reshape(8, P, 16)
        return (np.add.accumulate(m, axis=2) - m).reshape(8, NB)
    for t in range(T):
        now = [0] * N
        for q in range(N):
            s = (q + t) % N
            H = L[t % 2][q]; O = L[1 - t % 2][q]; C = ((H * O >> 5) + H + 37 * O) & (W - 1)
            h, o, c = [np.take_along_axis(X[s], v[:, None, :], 2) for v in (H, O, C)]
            zz = np.repeat(z[q], 16, axis=2); dh, do, dc = [np.add.reduce(np.abs(v - zz), axis=1) for v in (h, o, c)]
            live = H != O
            rec = live & (do <= np.minimum(dh, dc))
            want = live & ~rec & (dc < dh) & (G[q] < LG); am = want & (before(want) < CA)
            ins = live & ~rec & ~am
            ch = np.where(rec[:, None, :], o, np.where(am[:, None, :], c, h))
            V = np.add.reduce((ch - h).reshape(8, 16, P, 16), axis=3)
            ok = np.add.reduce((V >= 0).astype(np.int32), axis=1) >= LV
            now[s] = int(np.add.reduce((~ok).astype(np.int64), axis=None)); yes = np.repeat(ok, 16, axis=1)
            I[q] += ins | ((rec | am) & ~yes); G[q] += am & yes
            H2 = np.where(yes & rec, O, np.where(yes & am, C, H))
            sp = I[q] >= LI; v = np.where((before(sp) & 1) == 1, C, H)
            H2 = np.where(sp, v, H2); O2 = np.where(sp, v, O); I[q] = np.where(sp, 0, I[q])
            M = np.maximum.reduce(ch.reshape(8, 16, P, 16), axis=3); u = np.add.reduce(w[s] * M, axis=1) & (W - 1)
            O2 = np.where(live, O2, ((H * np.repeat(u, 16, axis=1) >> 5) + H + rej[s]) & (W - 1))
            L[t % 2][q] = H2; L[1 - t % 2][q] = O2
            if t < T - 1:
                z[q] = np.abs(z[q] - M)
                at = (S * np.arange(P)[None, :] + (u & (S - 1)))[:, None, :]
                np.put_along_axis(X[s], at, (np.take_along_axis(X[s], at, 2) + M) >> 1, 2)
        rej = now
    home = [(s - (T - 1)) % N for s in range(N)]
    ya, yb, yi, yg = [np.stack([gtable(m[q]) for q in home]).astype(np.float32) for m in (L[0], L[1], I, G)]
    return {"ya": ya, "yb": yb, "yi": yi, "yg": yg}

@@ -1,0 +1,550 @@
+from concourse.bass import DstId, RemoteDMATransfer
+from concourse.mybir import AluOpType, AxisListType, ActivationFunctionType
+
+OP = AluOpType
+AF = ActivationFunctionType
+W, NP, NREAD = 4096, 256, 6
+BLOCKS = [128, 128]
+SLOT = 128
+CY = 0.00083
+PECY = 0.0005
+PEO = 0.02
+VO = 0.05
+GR = 1.5
+WIN = 0.15
+PIECES = 2
+MODE = [{"h": "A", "o": "F", "c": "F"}, {"h": "A", "o": "F", "c": "F"}]
+LEADS = (0.0, 2.0, 3.0, 4.5, 6.0)
+PASSES = 25
+WAKE = 0.1
+NETT = 5.0
+
+DTY = {"aw": ("bfloat16", 2), "af": ("float32", 4), "ai": ("int32", 4), "au": ("uint16", 2), "ah": ("float16", 2)}
+_size = {k: 0 for k in DTY}
+
+
+def new(ar, n):
+    a = _size[ar]
+    step = 32 // DTY[ar][1]
+    _size[ar] = a + (n + step - 1) // step * step
+    return (ar, a, a + n, 1)
+
+
+def sub(h, a, b, s=1):
+    return (h[0], h[1] + a, h[1] + b, s)
+
+
+def ps(bank, slot, n):
+    return ("ps%d" % bank, slot * SLOT, slot * SLOT + n, 1)
+
+
+def ncol(h):
+    return (h[2] - h[1] + h[3] - 1) // h[3]
+
+
+def wide(h):
+    return 4 if h[0] not in DTY else DTY[h[0]][1]
+
+
+def build():
+    ops = []
+    NB = len(BLOCKS)
+    cur = [-1, 0]
+
+    def add(eng, cost, reads, writes, emit, name="", kind="c", sem=None, extra=()):
+        ops.append({"e": eng, "c": cost, "r": reads, "w": writes, "f": emit, "n": name, "k": kind, "s": sem, "x": list(extra), "t": cur[0], "blk": cur[1]})
+        return len(ops) - 1
+
+    def vts(o, i, s1, s2, op0, op1=None, name="ts"):
+        n = ncol(o)
+        fast = wide(o) == 2 and wide(i) == 2
+        rd = [i] + [s for s in (s1, s2) if isinstance(s, tuple)]
+
+        def f(q, V):
+            a = V(s1) if isinstance(s1, tuple) else s1
+            if op1 is None:
+                return q.tensor_scalar(V(o), V(i), a, None, op0)
+            b = V(s2) if isinstance(s2, tuple) else s2
+            return q.tensor_scalar(V(o), V(i), a, b, op0, op1)
+        return add("V", 0.03 + CY * max(64, n * (0.5 if fast else 1)), rd, [o], f, name)
+
+    def vtt(o, a, b, op, name="tt"):
+        n = ncol(o)
+        both = a[0] in DTY and b[0] in DTY
+        return add("V", 0.03 + CY * max(64, n * (2 if both else 1)), [a, b], [o], lambda q, V: q.tensor_tensor(V(o), V(a), V(b), op), name)
+
+    def vcopy(o, i, name="cp"):
+        n = ncol(o)
+        fast = wide(o) == 2 and wide(i) == 2
+        return add("V", 0.03 + CY * max(64, n * (0.5 if fast else 1)), [i], [o], lambda q, V: q.tensor_copy(V(o), V(i)), name)
+
+    def vset(o, v):
+        return add("V", 0.03 + CY * max(64, ncol(o) * (0.5 if wide(o) == 2 else 1)), [], [o], lambda q, V: q.memset(V(o), v), "set")
+
+    def act(o, i, fn, scale=1.0, bias=0.0, acc=None, name="act"):
+        def f(q, V):
+            if acc is None:
+                return q.activation(V(o), V(i), fn, bias, scale)
+            return q.activation(V(o), V(i), fn, bias, scale, accum_out=V(acc))
+        return add("A", 0.06 + CY * ncol(o), [i], [o] + ([acc] if acc else []), f, name)
+
+    def gath(eng, o, win, off, minus=None, op=None, name="gather"):
+        n = ncol(o)
+        if eng == "A":
+            return add("A", 0.07 + CY * GR * n, [win, off], [o],
+                       lambda q, V: q.activation(V(o), V(win).indirect(V(off)), AF.Copy), name)
+        if minus is None:
+            return add("V", 0.05 + CY * GR * n, [win, off], [o],
+                       lambda q, V: q.tensor_copy(V(o), V(win).indirect(V(off))), name)
+        return add("V", 0.05 + CY * GR * n, [win, off, minus], [o],
+                   lambda q, V: q.tensor_tensor(V(o), V(win).indirect(V(off)), V(minus), op), name)
+
+    def pe(o, terms, name="pe", first=True, stop=True, extra=()):
+        c = 0.03
+        for l, r in terms:
+            c += PEO + PECY * max(64, ncol(r)) * (4 if l[0] == "af" else 1)
+
+        def f(q, V):
+            last = None
+            for k, (l, r) in enumerate(terms):
+                last = q.matmul(V(o), V(l), V(r), first and k == 0, stop and k == len(terms) - 1)
+            return last
+        return add("P", c, [x for t in terms for x in t], [o], f, name, extra=[i for i in extra if i is not None])
+
+    def mailto(src, land, nm, t, b):
+        sem = "%s%d_%d" % (nm, t, b)
+        k = add("G", 1.0, [src], [], ("send", src, land, sem), nm, "send")
+        add("N", NETT, [], [land], None, nm, "net", sem, (k,))
+
+    X = new("aw", W)
+    xin, zin, win_ = X, new("aw", NP), new("aw", 1)
+    bain, bbin = new("ai", NP), new("ai", NP)
+    for k, (nm, h, q) in enumerate((("ba", bain, "S"), ("bb", bbin, "S"), ("zp", zin, "S"), ("wl", win_, "S"), ("xt", X, "S"))):
+        add(q, 0.1, [], [h], lambda q, V, nm=nm, h=h: q.dma_start(V(h), V(nm)), "ld" + nm, "dma", "ld" + nm)
+
+    ONE = new("aw", 128)
+    ID, NEG, BO, LT, L64, L4, T1 = [new("aw", 128) for _ in range(7)]
+    MID = {v: new("aw", 128) for v in (-64, -16, -2, 4, 2048, -4096, 528384)}
+    D, WD = new("aw", 144), new("aw", 144)
+    WB, WB64 = new("aw", 128), new("aw", 128)
+    HI, H65, H101 = [new("ah", 128) for _ in range(3)]
+    IF = new("af", 128)
+    NCM = max(BLOCKS) // 16
+    MASK = new("aw", 16 * max(BLOCKS))
+
+    def asel(o, i, pat, cmp, base, cm):
+        return add("G", 0.4, [i], [o], lambda q, V: q.affine_select(V(o), V(i), pat, cmp, 0.0, base, cm), "asel")
+    vset(ONE, 1.0)
+    asel(ID, ONE, [[-1, 128]], OP.is_equal, 0, 1)
+    asel(T1, ONE, [[-16, 8], [0, 16]], OP.is_ge, 0, 1)
+    asel(BO, T1, [[16, 8], [0, 16]], OP.is_ge, 15, -1)
+    asel(LT, BO, [[1, 128]], OP.is_gt, 0, -1)
+    B1, B2, BASE = new("ai", NCM), new("ai", NCM), new("ai", NCM)
+    add("G", 0.2, [], [B1], lambda q, V: q.iota(V(B1), [[0, NCM]], 0, 16), "iota")
+    add("G", 0.2, [], [B2], lambda q, V: q.iota(V(B2), [[256, NCM]], 0, 0), "iota")
+    vts(B1, B1, 255, None, OP.bitwise_and)
+    vtt(BASE, B1, B2, OP.add)
+    vcopy(HI, ID)
+    vts(H65, ID, 65.0, None, OP.mult)
+    vts(H101, ID, 101.0, None, OP.mult)
+    vts(NEG, ID, -1.0, None, OP.mult)
+    for v in sorted(MID):
+        act(MID[v], ID, AF.Copy, scale=float(v))
+    act(IF, ID, AF.Copy)
+    vtt(L64, LT, MID[-64], OP.add)
+    vtt(L4, LT, MID[4], OP.add)
+    vset(D, 0.0)
+    vcopy(sub(D, 15, 143, 16), sub(BO, 0, 128, 16))
+    WF = new("af", 1)
+    vcopy(WF, win_)
+    vts(WD, D, WF, None, OP.mult)
+    vts(WB, BO, WF, None, OP.mult)
+    vts(WB64, WB, 64.0, None, OP.mult)
+    vset(MASK, 1.0)
+    vset(sub(MASK, 0, 16 * max(BLOCKS), 16), 0.0)
+
+    p0 = [sum(BLOCKS[:b]) for b in range(NB)]
+    big = []
+    for b in range(NB):
+        n = BLOCKS[b]
+        d = {k: new("aw", 16 * n) for k in ("h", "o", "c", "ch", "ah", "zx", "zs")}
+        d.update({k: new("aw", n) for k in ("live", "rec", "want", "am", "sv", "jk", "ry", "ay", "spl", "fl", "so", "fu")})
+        d.update({k: new("ah", n) for k in ("Hc", "Oc", "Cc", "tO", "tC", "tH", "nHc", "s1", "s2")})
+        d.update({k: new("af", n) for k in ("dhS", "m", "gl", "dhG", "m2", "stU", "xg")})
+        d.update({k: new("ai", n) for k in ("P", "T", "C", "pU", "TU", "xf")})
+        d.update({k: new("ai", n // 16) for k in ("ui", "ua", "ul")})
+        d["C16"], d["ch16"], d["l16"] = new("au", n), new("au", n), new("au", n // 16)
+        vset(d["zs"], 0.0)
+        big.append(d)
+    ACC = new("af", 16 * NREAD)
+    RK = [new("af", 2) for _ in range(NREAD)]
+    RM = new("aw", 128)
+    subn = [0]
+    lastv = [None]
+
+    mail = []
+    for b in range(NB):
+        n = BLOCKS[b]
+        A16, B16, I0, G0 = new("au", n), new("au", n), new("aw", n), new("aw", n)
+        vcopy(A16, sub(bain, p0[b], p0[b] + n))
+        vcopy(B16, sub(bbin, p0[b], p0[b] + n))
+        vset(I0, 0.0)
+        vset(G0, 0.0)
+        mail.append((A16, B16, sub(zin, p0[b], p0[b] + n), I0, G0))
+
+    for t in range(NREAD):
+        last = t == NREAD - 1
+        nxt = []
+        for b in range(NB):
+            cur[0], cur[1] = t, b
+            n, d, par = BLOCKS[b], big[b], b & 1
+            H16, O16, z, I, G = mail[b][t & 1], mail[b][1 - (t & 1)], mail[b][2], mail[b][3], mail[b][4]
+            hp, lin = ps(2, 2 * par, n), ps(2, 2 * par + 1, n)
+            sg = ps(3 + par, 3, n)
+            vts(d["Hc"], H16, -2048.0, None, OP.add, name="Hc")
+            vts(d["Oc"], O16, -2048.0, None, OP.add, name="Oc")
+            pe(hp, [(HI, d["Hc"])], "HcPS")
+            pe(lin, [(H65, d["Hc"]), (H101, d["Oc"])], "lin")
+            vtt(d["P"], d["Oc"], hp, OP.mult, "P")
+            vts(d["P"], d["P"], 5, None, OP.arith_shift_right, name="P5")
+            vtt(d["T"], d["P"], lin, OP.add, "T")
+            vts(d["C"], d["T"], 4095, None, OP.bitwise_and, name="C")
+            vcopy(d["C16"], d["C"], "C16")
+            vts(d["Cc"], d["C16"], -2048.0, None, OP.add, name="Cc")
+            vtt(d["live"], d["Oc"], hp, OP.not_equal, "live")
+            act(sub(d["zs"], 0, 16 * n, 16), z, AF.Copy, name="zs")
+            mk = sub(MASK, 0, 16 * n)
+            add("V", 0.03 + CY * 8 * n, [mk, d["zs"]], [d["zx"]],
+                lambda q, V, mk=mk, d=d: q.tensor_tensor_scan(V(d["zx"]), V(mk), V(d["zs"]), 0.0, OP.mult, OP.add), "zx")
+            act(sg, G, AF.Sign, scale=-1.0, bias=1.5, name="sg")
+            vtt(d["gl"], d["live"], sg, OP.mult, "gl")
+        for b in range(NB):
+            cur[0], cur[1] = t, b
+            n, d, par = BLOCKS[b], big[b], b & 1
+            H16, O16, z, I, G = mail[b][t & 1], mail[b][1 - (t & 1)], mail[b][2], mail[b][3], mail[b][4]
+            dh, do, dc, cap = [ps(3 + par, k, n) for k in range(4)]
+            vs = ps(5, b, n)
+            pc = [(k * n // PIECES, (k + 1) * n // PIECES) for k in range(PIECES)]
+            for k, lst, dist in (("h", H16, dh), ("o", O16, do), ("c", d["C16"], dc)):
+                res = d["ah"] if k == "h" else d[k]
+                for q0, q1 in pc:
+                    e0, e1 = 16 * q0, 16 * q1
+                    if MODE[b][k] == "F":
+                        gath("V", sub(d[k], e0, e1), X, sub(lst, q0, q1), sub(d["zx"], e0, e1), OP.subtract, k)
+                        act(sub(res, e0, e1), sub(d[k], e0, e1), AF.Abs, name="abs" + k)
+                        continue
+                    gath(MODE[b][k], sub(d[k], e0, e1), X, sub(lst, q0, q1), name=k)
+                    for a0 in range(e0, e1, 512):
+                        a1 = min(a0 + 512, e1)
+                        tile = ("ps%d" % (subn[0] & 1), 0, a1 - a0, 1)
+                        subn[0] += 1
+                        pe(tile, [(ID, sub(d[k], a0, a1)), (NEG, sub(d["zx"], a0, a1))], "sub")
+                        act(sub(res, a0, a1), tile, AF.Abs, name="abs" + k)
+                pe(dist, [(sub(D, 15 - j, 143 - j), sub(res, j, 16 * n, 16)) for j in range(16)], "d" + k)
+                if k == "h":
+                    pe(vs, [(NEG, sub(d["h"], j, 16 * n, 16)) for j in range(16)] + ([(MID[-16], z)] if MODE[b]["h"] == "F" else []), "voteh", stop=False, extra=lastv)
+            act(d["dhS"], dh, AF.Copy, name="dhS")
+            vtt(d["dhG"], d["gl"], dh, OP.mult, "dhG")
+            vtt(d["m2"], d["dhG"], do, OP.min, "m2")
+            vtt(d["m"], d["dhS"], dc, OP.min, "m")
+            vtt(d["want"], d["m2"], dc, OP.is_gt, "want")
+            vtt(d["rec"], d["m"], do, OP.is_ge, "rec")
+            pe(cap, [(L64, d["want"])], "cap")
+            vts(d["am"], cap, -60.0, None, OP.is_lt, name="am")
+            rp, ap_, sp_, cs = dh, do, dc, cap
+            pe(rp, [(ID, d["rec"])], "recPS")
+            vtt(d["tO"], d["Oc"], rp, OP.mult, "tO")
+            pe(ap_, [(ID, d["am"])], "amPS")
+            pe(sp_, [(ID, sub(ONE, 0, n)), (NEG, d["rec"]), (NEG, d["am"])], "sH")
+            vtt(d["tC"], d["Cc"], ap_, OP.mult, "tC")
+            vtt(d["tH"], d["Hc"], sp_, OP.mult, "tH")
+            pe(cs, [(HI, d["tO"]), (HI, d["tC"]), (HI, d["tH"])], "chS")
+            vts(d["ch16"], cs, 2048.0, None, OP.add, name="ch16")
+            for q0, q1 in pc:
+                gath("A", sub(d["ch"], 16 * q0, 16 * q1), X, sub(d["ch16"], q0, q1), name="ch")
+            lastv[0] = pe(vs, [(ID, sub(d["ch"], j, 16 * n, 16)) for j in range(16)], "vote", first=False)
+        for b in range(NB):
+            cur[0], cur[1] = t, b
+            n, d, par = BLOCKS[b], big[b], b & 1
+            z = mail[b][2]
+            mx = d["zx"]
+            for k in range(PIECES):
+                q0, q1 = 16 * (k * n // PIECES), 16 * ((k + 1) * n // PIECES)
+                mk, cp, mp = sub(MASK, 0, q1 - q0), sub(d["ch"], q0, q1), sub(mx, q0, q1)
+                add("V", VO + CY * (q1 - q0) / 2, [mk, cp], [mp],
+                    lambda q, V, mk=mk, cp=cp, mp=mp: q.tensor_tensor_scan(V(mp), V(mk), V(cp), 0.0, OP.mult, OP.max), "mx")
+            M = sub(mx, 15, 16 * n, 16)
+            ur, uc = ps(6, 2 * par, n), ps(6, 2 * par + 1, n)
+            d["M"], d["ur"], d["uc"] = M, ur, uc
+            out = {}
+            if not last:
+                out["AB"] = new("au", 2 * n)
+                out["ZIG"] = new("aw", 3 * n)
+                out["A"], out["B"] = sub(out["AB"], 0, n), sub(out["AB"], n, 2 * n)
+                out["z"], out["I"], out["G"] = [sub(out["ZIG"], k * n, (k + 1) * n) for k in range(3)]
+                ulp = sub(uc, 0, n // 16)
+                pe(ulp, [(sub(WD, 15 - j, 143 - j), sub(mx, 15 + 16 * j, 16 * n, 256)) for j in range(16)], "ulist")
+                vcopy(d["ui"], ulp, "ui")
+                vts(d["ua"], d["ui"], 15, None, OP.bitwise_and, name="ua")
+                vtt(d["ul"], d["ua"], sub(BASE, 0, n // 16), OP.add, "ul")
+                vcopy(d["l16"], d["ul"], "l16")
+                xw = sub(X, 16 * p0[b], 16 * (p0[b] + n))
+                gath("V", d["xg"], xw, d["l16"], M, OP.add, "xg")
+                vts(d["xf"], d["xg"], -0.5, 0.5, OP.add, OP.mult, name="xf")
+                add("V", 0.05 + CY * 3.8 * n, [d["xf"], d["l16"]], [xw],
+                    lambda q, V, d=d, xw=xw: q.tensor_copy(V(xw).indirect(V(d["l16"])), V(d["xf"])), "scat")
+            else:
+                out["A"], out["B"], out["I"], out["G"] = [new("af", n) for _ in range(4)]
+            d["out"] = out
+        for b in range(NB):
+            cur[0], cur[1] = t, b
+            n, d, par = BLOCKS[b], big[b], b & 1
+            H16, O16, z, I, G = mail[b][t & 1], mail[b][1 - (t & 1)], mail[b][2], mail[b][3], mail[b][4]
+            out, M, ur, uc = d["out"], d["M"], d["ur"], d["uc"]
+            one = sub(ONE, 0, n)
+            S0, S1, S2, S3 = [ps(3 + par, k, n) for k in range(4)]
+            vs, cn = ps(5, b, n), S3
+            old0, old1 = ps(2, 2 * par, n), ps(2, 2 * par + 1, n)
+            yes, nm = ps(7, 2 * par, n), ps(7, 2 * par + 1, n)
+            act(d["sv"], vs, AF.Sign, bias=0.5, name="sv")
+            pe(cn, [(BO, d["sv"])], "cnt")
+            vts(yes, cn, 0.0, None, OP.is_ge, name="yes")
+            if not last:
+                act(d["jk"], cn, AF.Sign, bias=0.5, acc=sub(ACC, 16 * t + b, 16 * t + b + 1), name="rej")
+                pe(old1, [(ID, z), (NEG, M)], "zd")
+                act(out["z"], old1, AF.Abs, name="z")
+            vtt(d["ry"], d["rec"], yes, OP.mult, "ry")
+            vtt(d["ay"], d["am"], yes, OP.mult, "ay")
+            pe(old0, [(ID, G), (ID, d["ay"])], "Gs")
+            act(out["G"], old0, AF.Copy, name="G")
+            pe(S0, [(ID, d["ry"]), (ID, d["ay"])], "mv")
+            vtt(nm, d["live"], S0, OP.is_gt, "nm")
+            vtt(out["I"], I, nm, OP.not_equal, "I")
+            vtt(d["spl"], I, nm, OP.mult, "spl")
+            if not last:
+                zl, lh, lo = new("aw", 3 * n), new("au", n), new("au", n)
+                mailto(out["ZIG"], zl, "rz", t, b)
+            pe(S1, [(LT, d["spl"])], "bef")
+            act(d["fl"], S1, AF.Copy, scale=0.5, bias=128.75, name="fl")
+            pe(S2, [(L4, d["spl"]), (MID[-2], d["fl"])], "par")
+            vts(d["so"], S2, -253.5, None, OP.is_gt, name="so")
+            pe(S3, [(ID, one), (NEG, d["ry"]), (NEG, d["ay"]), (NEG, d["so"])], "sH2")
+            pe(S0, [(ID, d["ay"]), (ID, d["so"])], "a2")
+            vtt(d["tO"], d["tO"], yes, OP.mult, "tO2")
+            vtt(d["tC"], d["Cc"], S0, OP.mult, "tC2")
+            vtt(d["tH"], d["Hc"], S3, OP.mult, "tH2")
+            pe(S1, [(HI, d["tO"]), (HI, d["tC"]), (HI, d["tH"])], "nHs")
+            oh, oo = (out["A"], out["B"]) if t % 2 == 0 else (out["B"], out["A"])
+            vts(oh, S1, 2048.0, None, OP.add, name="nH")
+            if not last:
+                mailto(oh, lh, "rh", t, b)
+            pe(ur, [(WB, M)], "uraw")
+            act(d["fu"], ur, AF.Copy, scale=1.0 / 4096, bias=128.5 + 1.0 / 8192, name="fu")
+            pe(uc, [(MID[528384], one), (MID[-4096], d["fu"]), (WB, M)], "u")
+            lin = [(HI, d["Hc"]), (WB64, M), (MID[2048], one)]
+            if t > 0:
+                lin.append((RM, one))
+            vtt(d["pU"], d["Hc"], uc, OP.mult, "pU")
+            vts(d["pU"], d["pU"], 5, None, OP.arith_shift_right, name="pU5")
+            pe(ur, lin, "linU")
+            vtt(d["TU"], d["pU"], ur, OP.add, "TU")
+            vts(d["TU"], d["TU"], 4095, None, OP.bitwise_and, name="U")
+            vts(d["nHc"], oh, -2048.0, None, OP.add, name="nHc")
+            pe(S2, [(ID, d["spl"])], "splPS")
+            pe(S3, [(ID, d["live"]), (NEG, d["spl"])], "sO")
+            pe(S0, [(ID, one), (NEG, d["live"])], "st")
+            vtt(d["stU"], d["TU"], S0, OP.mult, "stU")
+            vtt(d["s2"], d["Oc"], S3, OP.mult, "s2")
+            vtt(d["s1"], d["nHc"], S2, OP.mult, "s1")
+            pe(S1, [(MID[2048], d["live"]), (IF, d["stU"]), (HI, d["s2"]), (HI, d["s1"])], "nOs")
+            vcopy(oo, S1, "nO")
+            if not last:
+                mailto(oo, lo, "ro", t, b)
+                nxt.append(((lh, lo) if t % 2 == 0 else (lo, lh)) + (sub(zl, 0, n), sub(zl, n, 2 * n), sub(zl, 2 * n, 3 * n)))
+            else:
+                for k, nme in (("G", "yg"), ("I", "yi"), ("A", "ya"), ("B", "yb")):
+                    add("S", 0.1, [out[k]], [], lambda q, V, nme=nme, h=out[k], a=p0[b], n=n: q.dma_start(V(nme)[:, a:a + n], V(h)), "st" + nme, "dma", "st%s%d" % (nme, b))
+        if not last:
+            acc, r = sub(ACC, 16 * t, 16 * t + NB), RK[t]
+            r0, r1 = sub(r, 0, 1), sub(r, 1, 2)
+            add("V", 0.1, [acc], [r0], lambda q, V, acc=acc, r0=r0: q.tensor_reduce(V(r0), V(acc), AxisListType.X, OP.add), "red")
+            vts(r1, r0, -1.0 / 32, 8.0, OP.mult, OP.add, name="rk")
+            vts(RM, ONE, r1, None, OP.mult, name="RM")
+        mail = nxt
+    return ops
+
+
+def depend(ops):
+    hist = {}
+    for i, o in enumerate(ops):
+        dep = set(o["x"])
+        for h, w in [(h, 0) for h in o["r"]] + [(h, 1) for h in o["w"]]:
+            for j, a, b, jw in hist.get(h[0], ()):
+                if (w or jw) and a < h[2] and h[1] < b:
+                    dep.add(j)
+        for h, w in [(h, 0) for h in o["r"]] + [(h, 1) for h in o["w"]]:
+            lst = hist.setdefault(h[0], [])
+            if w:
+                lst[:] = [e for e in lst if not (h[1] <= e[1] and e[2] <= h[2] and h[3] == 1)]
+            lst.append((i, h[1], h[2], w))
+        dep.discard(i)
+        o["d"] = sorted(dep)
+        o["b"] = sorted({h[0] for h in o["r"] + o["w"] if h[0] not in DTY})
+
+
+LDT = {"ldba": 3.0, "ldbb": 3.2, "ldzp": 3.4, "ldwl": 3.4, "ldxt": 7.0}
+
+
+def schedule(ops, pri, pred, succ):
+    n = len(ops)
+    left = [len(p) for p in pred]
+    ready = {}
+    est = [0.0] * n
+    free, bank = {}, {}
+    end, start = [0.0] * n, [0.0] * n
+    for i in range(n):
+        if not left[i]:
+            ready.setdefault(ops[i]["e"], []).append(i)
+    order, done = [], 0
+    while done < n:
+        best = None
+        for e, lst in ready.items():
+            if not lst:
+                continue
+            t0 = free.get(e, 0.0) if e != "N" else 0.0
+            cand = []
+            for i in lst:
+                s = max(t0, est[i])
+                for b in ops[i]["b"]:
+                    for e2, u in bank.get(b, {}).items():
+                        if e2 != e:
+                            s = max(s, u + WAKE)
+                cand.append((s, -pri[i], i))
+            s0 = min(cand)[0]
+            c = min((c for c in cand if c[0] <= s0 + WIN), key=lambda c: c[1])
+            if best is None or c[0] < best[0]:
+                best = (c[0], c[2], e)
+        s, i, e = best
+        ready[e].remove(i)
+        o = ops[i]
+        start[i] = s
+        end[i] = s + o["c"]
+        fin = end[i]
+        if o["k"] == "dma":
+            fin = s + LDT.get(o["n"], 2.5)
+        free[e] = end[i]
+        for b in o["b"]:
+            bank.setdefault(b, {})[e] = end[i]
+        order.append(i)
+        done += 1
+        for j in succ[i]:
+            est[j] = max(est[j], fin + (WAKE if ops[j]["e"] != e else 0.06))
+            left[j] -= 1
+            if not left[j]:
+                ready.setdefault(ops[j]["e"], []).append(j)
+        end[i] = fin
+    return order, start, end
+
+
+def plan(ops):
+    n = len(ops)
+    pred = [o["d"] for o in ops]
+    succ = [[] for _ in ops]
+    for i in range(n):
+        for j in pred[i]:
+            succ[j].append(i)
+    path = [0.0] * n
+    for i in range(n - 1, -1, -1):
+        path[i] = ops[i]["c"] + max([path[j] + WAKE for j in succ[i]], default=0.0)
+    best = None
+    for lead in LEADS:
+        pri = [p + (lead if o["t"] >= 0 and o["blk"] == 0 else 0.0) for p, o in zip(path, ops)]
+        for _ in range(PASSES):
+            order, start, end = schedule(ops, pri, pred, succ)
+            if best is None or max(end) < max(best[2]):
+                best = (order, start, end)
+            back = schedule(ops, end, succ, pred)[2]
+            pri = back
+    return best
+
+
+OPS = build()
+depend(OPS)
+ORDER, START, END = plan(OPS)
+
+SCRATCH = {k: ("sbuf", [128, _size[k]], DTY[k][0]) for k in DTY}
+SCRATCH.update({"ps%d" % k: ("psum", [128, 512], "float32") for k in range(8)})
+SEMAPHORES = ["cV", "cA", "cP", "cG", "sent"] + sorted({o["s"] for o in OPS if o["s"]})
+
+
+def rank_program(g, core, T, topo):
+    rank = T.rank_of(core)
+    if rank is None:
+        return
+    dst = T.cores[(rank + 1) % len(T.cores)]
+    rid, pid, _ = topo.addr(dst)
+    mask = topo.mask(core, dst)
+    width = len(topo.engines(core, dst))
+    queue = {"V": g.vector, "A": g.scalar, "P": g.tensor, "G": g, "S": g.sync}
+
+    def V(h):
+        if isinstance(h, str):
+            return T[h][:]
+        if h[3] == 1:
+            return T[h[0]][:, h[1]:h[2]]
+        return T[h[0]][:, h[1]:h[2]:h[3]]
+
+    count = {e: 0 for e in "VAPG"}
+    know = {e: {} for e in queue}
+    snap = {}
+    lastb = {}
+    sent = 0
+    sig = {}
+
+    def need(e, i):
+        s, c = sig[i]
+        if know[e].get(s, 0) >= c:
+            return
+        queue[e].wait_ge(T.sem[s], c)
+        for k, v in snap[i].items():
+            if know[e].get(k, 0) < v:
+                know[e][k] = v
+        know[e][s] = c
+
+    for i in ORDER:
+        o = OPS[i]
+        e = o["e"]
+        if o["k"] == "net":
+            sig[i] = (o["s"], width)
+            snap[i] = {}
+            continue
+        deps = {j for j in o["d"] if OPS[j]["k"] != "send"}
+        for b in o["b"]:
+            for e2, j in lastb.get(b, {}).items():
+                if e2 != e:
+                    deps.add(j)
+        for j in sorted(deps, key=lambda j: -START[j]):
+            need(e, j)
+        if o["k"] == "send":
+            _s, src, land, sem = o["f"]
+            g.remote_dma(V(land), V(src), T.sem[sem], T.sem.sent, pid, rid, mask)
+            sent += width
+            continue
+        ins = o["f"](queue[e], V)
+        if o["k"] == "dma":
+            ins.then_inc(T.sem[o["s"]], 16)
+            sig[i] = (o["s"], 16)
+            snap[i] = dict(know[e])
+        else:
+            count[e] += 1
+            ins.then_inc(T.sem["c" + e], 1)
+            sig[i] = ("c" + e, count[e])
+            snap[i] = dict(know[e])
+            for b in o["b"]:
+                lastb.setdefault(b, {})[e] = i
+    for e in "VAPG":
+        g.wait_ge(T.sem["c" + e], count[e])
+    for i in ORDER:
+        if OPS[i]["k"] in ("dma", "net"):
+            g.wait_ge(T.sem[OPS[i]["s"]], sig[i][1])
+    g.wait_ge(T.sem.sent, sent)

@@ -7,13 +7,18 @@ W, NP, NREAD = 4096, 256, 6
 BLOCKS = [128, 128]
 SLOT = 128
 CY = 0.00083
-PECY = 0.0005
+PECY = 0.00042
 PEO = 0.02
 VO = 0.05
-GR = 1.5
+GR = 1.6
 WIN = 0.15
 PIECES = 2
-MODE = [{"h": "A", "o": "F", "c": "F"}, {"h": "A", "o": "F", "c": "F"}]
+MODE = [{"h": "AA", "o": "FF", "c": "FF"}, {"h": "AA", "o": "FF", "c": "FF"}]
+CHQ = ["AV", "AV"]
+SPLIT = "c"
+VH = 8
+SEED = 1
+NOISE = 0.0
 LEADS = (0.0, 2.0, 3.0, 4.5, 6.0)
 PASSES = 25
 WAKE = 0.1
@@ -124,10 +129,11 @@ def build():
 
     ONE = new("aw", 128)
     ID, NEG, BO, LT, L64, L4, T1 = [new("aw", 128) for _ in range(7)]
-    MID = {v: new("aw", 128) for v in (-64, -16, -2, 4, 2048, -4096, 528384)}
+    MID = {v: new("aw", 128) for v in (-64, -2, 4, 2048, -4096, 528384, -2 ** 23, 2 ** 30, 65536, 98304)}
     D, WD = new("aw", 144), new("aw", 144)
     WB, WB64 = new("aw", 128), new("aw", 128)
-    HI, H65, H101 = [new("ah", 128) for _ in range(3)]
+    HI, H65, H101, H32, HH = [new("ah", 128) for _ in range(5)]
+    MONE = new("aw", max(BLOCKS))
     IF = new("af", 128)
     NCM = max(BLOCKS) // 16
     MASK = new("aw", 16 * max(BLOCKS))
@@ -145,8 +151,9 @@ def build():
     vts(B1, B1, 255, None, OP.bitwise_and)
     vtt(BASE, B1, B2, OP.add)
     vcopy(HI, ID)
-    vts(H65, ID, 65.0, None, OP.mult)
-    vts(H101, ID, 101.0, None, OP.mult)
+    vts(H65, ID, 2080.0, None, OP.mult)
+    vts(H101, ID, 3232.0, None, OP.mult)
+    vts(H32, ID, 32.0, None, OP.mult)
     vts(NEG, ID, -1.0, None, OP.mult)
     for v in sorted(MID):
         act(MID[v], ID, AF.Copy, scale=float(v))
@@ -159,7 +166,9 @@ def build():
     vcopy(WF, win_)
     vts(WD, D, WF, None, OP.mult)
     vts(WB, BO, WF, None, OP.mult)
-    vts(WB64, WB, 64.0, None, OP.mult)
+    vts(WB64, WB, 2048.0, None, OP.mult)
+    vset(MONE, -1.0)
+    vts(HH, ID, 0.5, None, OP.mult)
     vset(MASK, 1.0)
     vset(sub(MASK, 0, 16 * max(BLOCKS), 16), 0.0)
 
@@ -169,16 +178,15 @@ def build():
         n = BLOCKS[b]
         d = {k: new("aw", 16 * n) for k in ("h", "o", "c", "ch", "ah", "zx", "zs")}
         d.update({k: new("aw", n) for k in ("live", "rec", "want", "am", "sv", "jk", "ry", "ay", "spl", "fl", "so", "fu")})
-        d.update({k: new("ah", n) for k in ("Hc", "Oc", "Cc", "tO", "tC", "tH", "nHc", "s1", "s2")})
-        d.update({k: new("af", n) for k in ("dhS", "m", "gl", "dhG", "m2", "stU", "xg")})
-        d.update({k: new("ai", n) for k in ("P", "T", "C", "pU", "TU", "xf")})
+        d.update({k: new("ah", n) for k in ("Hc", "Oc", "Cc", "tO", "tC", "tH", "s1", "s2")})
+        d.update({k: new("af", n) for k in ("dhS", "m", "gl", "dhG", "m2", "stU", "xg", "P", "pU")})
+        d.update({k: new("ai", n) for k in ("T", "C", "TU", "xf")})
         d.update({k: new("ai", n // 16) for k in ("ui", "ua", "ul")})
         d["C16"], d["ch16"], d["l16"] = new("au", n), new("au", n), new("au", n // 16)
         vset(d["zs"], 0.0)
         big.append(d)
     ACC = new("af", 16 * NREAD)
-    RK = [new("af", 2) for _ in range(NREAD)]
-    RM = new("aw", 128)
+    RM = [[new("aw", 128) for _ in range(NB)] for _ in range(2)] * 3
     subn = [0]
     lastv = [None]
 
@@ -206,9 +214,8 @@ def build():
             pe(hp, [(HI, d["Hc"])], "HcPS")
             pe(lin, [(H65, d["Hc"]), (H101, d["Oc"])], "lin")
             vtt(d["P"], d["Oc"], hp, OP.mult, "P")
-            vts(d["P"], d["P"], 5, None, OP.arith_shift_right, name="P5")
             vtt(d["T"], d["P"], lin, OP.add, "T")
-            vts(d["C"], d["T"], 4095, None, OP.bitwise_and, name="C")
+            vts(d["C"], d["T"], 5, 4095, OP.arith_shift_right, OP.bitwise_and, name="C")
             vcopy(d["C16"], d["C"], "C16")
             vts(d["Cc"], d["C16"], -2048.0, None, OP.add, name="Cc")
             vtt(d["live"], d["Oc"], hp, OP.not_equal, "live")
@@ -227,22 +234,25 @@ def build():
             pc = [(k * n // PIECES, (k + 1) * n // PIECES) for k in range(PIECES)]
             for k, lst, dist in (("h", H16, dh), ("o", O16, do), ("c", d["C16"], dc)):
                 res = d["ah"] if k == "h" else d[k]
-                for q0, q1 in pc:
+                for (q0, q1), mode in zip(pc, MODE[b][k]):
                     e0, e1 = 16 * q0, 16 * q1
-                    if MODE[b][k] == "F":
+                    if mode == "F":
                         gath("V", sub(d[k], e0, e1), X, sub(lst, q0, q1), sub(d["zx"], e0, e1), OP.subtract, k)
                         act(sub(res, e0, e1), sub(d[k], e0, e1), AF.Abs, name="abs" + k)
                         continue
-                    gath(MODE[b][k], sub(d[k], e0, e1), X, sub(lst, q0, q1), name=k)
+                    gath(mode, sub(d[k], e0, e1), X, sub(lst, q0, q1), name=k)
                     for a0 in range(e0, e1, 512):
                         a1 = min(a0 + 512, e1)
                         tile = ("ps%d" % (subn[0] & 1), 0, a1 - a0, 1)
                         subn[0] += 1
                         pe(tile, [(ID, sub(d[k], a0, a1)), (NEG, sub(d["zx"], a0, a1))], "sub")
                         act(sub(res, a0, a1), tile, AF.Abs, name="abs" + k)
-                pe(dist, [(sub(D, 15 - j, 143 - j), sub(res, j, 16 * n, 16)) for j in range(16)], "d" + k)
+                for q0, q1 in (pc if k in SPLIT else [(0, n)]):
+                    pe(sub(dist, q0, q1), [(sub(D, 15 - j, 143 - j), sub(res, 16 * q0 + j, 16 * q1, 16)) for j in range(16)], "d" + k)
                 if k == "h":
-                    pe(vs, [(NEG, sub(d["h"], j, 16 * n, 16)) for j in range(16)] + ([(MID[-16], z)] if MODE[b]["h"] == "F" else []), "voteh", stop=False, extra=lastv)
+                    for j0 in range(0, 16, VH):
+                        terms = [(NEG, sub(d["h"], j, 16 * n, 16)) for j in range(j0, j0 + VH)]
+                        pe(vs, terms, "voteh", first=j0 == 0, stop=False, extra=lastv)
             act(d["dhS"], dh, AF.Copy, name="dhS")
             vtt(d["dhG"], d["gl"], dh, OP.mult, "dhG")
             vtt(d["m2"], d["dhG"], do, OP.min, "m2")
@@ -260,8 +270,8 @@ def build():
             vtt(d["tH"], d["Hc"], sp_, OP.mult, "tH")
             pe(cs, [(HI, d["tO"]), (HI, d["tC"]), (HI, d["tH"])], "chS")
             vts(d["ch16"], cs, 2048.0, None, OP.add, name="ch16")
-            for q0, q1 in pc:
-                gath("A", sub(d["ch"], 16 * q0, 16 * q1), X, sub(d["ch16"], q0, q1), name="ch")
+            for (q0, q1), e in zip(pc, CHQ[b]):
+                gath(e, sub(d["ch"], 16 * q0, 16 * q1), X, sub(d["ch16"], q0, q1), name="ch")
             lastv[0] = pe(vs, [(ID, sub(d["ch"], j, 16 * n, 16)) for j in range(16)], "vote", first=False)
         for b in range(NB):
             cur[0], cur[1] = t, b
@@ -308,13 +318,15 @@ def build():
             yes, nm = ps(7, 2 * par, n), ps(7, 2 * par + 1, n)
             act(d["sv"], vs, AF.Sign, bias=0.5, name="sv")
             pe(cn, [(BO, d["sv"])], "cnt")
-            vts(yes, cn, 0.0, None, OP.is_ge, name="yes")
+            acc = sub(ACC, 16 * t + b, 16 * t + b + 1)
+            act(yes, cn, AF.Sign, bias=0.5, acc=None if last else acc, name="yes")
             if not last:
-                act(d["jk"], cn, AF.Sign, bias=0.5, acc=sub(ACC, 16 * t + b, 16 * t + b + 1), name="rej")
+                rm = RM[t][b]
+                add("A", 0.06 + CY * 128, [ONE, acc], [rm], lambda q, V, rm=rm, acc=acc: q.activation(V(rm), V(ONE), AF.Copy, 0.0, V(acc)), "RM")
                 pe(old1, [(ID, z), (NEG, M)], "zd")
                 act(out["z"], old1, AF.Abs, name="z")
-            vtt(d["ry"], d["rec"], yes, OP.mult, "ry")
-            vtt(d["ay"], d["am"], yes, OP.mult, "ay")
+            vtt(d["ry"], d["rec"], yes, OP.is_equal, "ry")
+            vtt(d["ay"], d["am"], yes, OP.is_equal, "ay")
             pe(old0, [(ID, G), (ID, d["ay"])], "Gs")
             act(out["G"], old0, AF.Copy, name="G")
             pe(S0, [(ID, d["ry"]), (ID, d["ay"])], "mv")
@@ -330,10 +342,10 @@ def build():
             vts(d["so"], S2, -253.5, None, OP.is_gt, name="so")
             pe(S3, [(ID, one), (NEG, d["ry"]), (NEG, d["ay"]), (NEG, d["so"])], "sH2")
             pe(S0, [(ID, d["ay"]), (ID, d["so"])], "a2")
-            vtt(d["tO"], d["tO"], yes, OP.mult, "tO2")
+            vtt(d["s1"], d["tO"], yes, OP.mult, "tO2")
             vtt(d["tC"], d["Cc"], S0, OP.mult, "tC2")
             vtt(d["tH"], d["Hc"], S3, OP.mult, "tH2")
-            pe(S1, [(HI, d["tO"]), (HI, d["tC"]), (HI, d["tH"])], "nHs")
+            pe(S1, [(HH, d["tO"]), (HH, d["s1"]), (HI, d["tC"]), (HI, d["tH"])], "nHs")
             oh, oo = (out["A"], out["B"]) if t % 2 == 0 else (out["B"], out["A"])
             vts(oh, S1, 2048.0, None, OP.add, name="nH")
             if not last:
@@ -341,35 +353,26 @@ def build():
             pe(ur, [(WB, M)], "uraw")
             act(d["fu"], ur, AF.Copy, scale=1.0 / 4096, bias=128.5 + 1.0 / 8192, name="fu")
             pe(uc, [(MID[528384], one), (MID[-4096], d["fu"]), (WB, M)], "u")
-            lin = [(HI, d["Hc"]), (WB64, M), (MID[2048], one)]
+            lin = [(WB64, M), (MID[-2 ** 23], d["fu"]), (MID[2 ** 30], one), (H32, d["Hc"]), (MID[98304 if t else 65536], one)]
             if t > 0:
-                lin.append((RM, one))
+                lin += [(RM[t - 1][k], sub(MONE, 0, n)) for k in range(NB)]
             vtt(d["pU"], d["Hc"], uc, OP.mult, "pU")
-            vts(d["pU"], d["pU"], 5, None, OP.arith_shift_right, name="pU5")
             pe(ur, lin, "linU")
             vtt(d["TU"], d["pU"], ur, OP.add, "TU")
-            vts(d["TU"], d["TU"], 4095, None, OP.bitwise_and, name="U")
-            vts(d["nHc"], oh, -2048.0, None, OP.add, name="nHc")
-            pe(S2, [(ID, d["spl"])], "splPS")
+            vts(d["TU"], d["TU"], 5, 4095, OP.arith_shift_right, OP.bitwise_and, name="U")
             pe(S3, [(ID, d["live"]), (NEG, d["spl"])], "sO")
             pe(S0, [(ID, one), (NEG, d["live"])], "st")
             vtt(d["stU"], d["TU"], S0, OP.mult, "stU")
             vtt(d["s2"], d["Oc"], S3, OP.mult, "s2")
-            vtt(d["s1"], d["nHc"], S2, OP.mult, "s1")
-            pe(S1, [(MID[2048], d["live"]), (IF, d["stU"]), (HI, d["s2"]), (HI, d["s1"])], "nOs")
-            vcopy(oo, S1, "nO")
+            vtt(d["s1"], d["spl"], S1, OP.mult, "s1")
+            pe(S2, [(MID[2048], d["live"]), (IF, d["stU"]), (HI, d["s2"]), (HI, d["s1"])], "nOs")
+            vcopy(oo, S2, "nO")
             if not last:
                 mailto(oo, lo, "ro", t, b)
                 nxt.append(((lh, lo) if t % 2 == 0 else (lo, lh)) + (sub(zl, 0, n), sub(zl, n, 2 * n), sub(zl, 2 * n, 3 * n)))
             else:
                 for k, nme in (("G", "yg"), ("I", "yi"), ("A", "ya"), ("B", "yb")):
                     add("S", 0.1, [out[k]], [], lambda q, V, nme=nme, h=out[k], a=p0[b], n=n: q.dma_start(V(nme)[:, a:a + n], V(h)), "st" + nme, "dma", "st%s%d" % (nme, b))
-        if not last:
-            acc, r = sub(ACC, 16 * t, 16 * t + NB), RK[t]
-            r0, r1 = sub(r, 0, 1), sub(r, 1, 2)
-            add("V", 0.1, [acc], [r0], lambda q, V, acc=acc, r0=r0: q.tensor_reduce(V(r0), V(acc), AxisListType.X, OP.add), "red")
-            vts(r1, r0, -1.0 / 32, 8.0, OP.mult, OP.add, name="rk")
-            vts(RM, ONE, r1, None, OP.mult, name="RM")
         mail = nxt
     return ops
 
@@ -457,6 +460,12 @@ def plan(ops):
     for i in range(n - 1, -1, -1):
         path[i] = ops[i]["c"] + max([path[j] + WAKE for j in succ[i]], default=0.0)
     best = None
+    seed = [SEED]
+
+    def rnd():
+        seed[0] = (seed[0] * 1103515245 + 12345) % 2147483648
+        return seed[0] / 1073741824.0 - 1.0
+
     for lead in LEADS:
         pri = [p + (lead if o["t"] >= 0 and o["blk"] == 0 else 0.0) for p, o in zip(path, ops)]
         for _ in range(PASSES):
@@ -464,7 +473,7 @@ def plan(ops):
             if best is None or max(end) < max(best[2]):
                 best = (order, start, end)
             back = schedule(ops, end, succ, pred)[2]
-            pri = back
+            pri = [x + NOISE * rnd() for x in back]
     return best
 
 

from concourse.bass import DstId, RemoteDMATransfer
from concourse.mybir import AluOpType, AxisListType, ActivationFunctionType

OP = AluOpType
AF = ActivationFunctionType
W, NP, NREAD = 4096, 256, 6
BLOCKS = [128, 128]
SLOT = 128
CY = 0.00083
PECY = 0.00042
PEO = 0.02
VO = 0.05
GR = 1.6
WIN = 0.15
PIECES = 2
MODE = [{"h": "AA", "o": "FF", "c": "FF"}, {"h": "AA", "o": "FF", "c": "FF"}]
CHQ = ["AV", "AV"]
SPLIT = "c"
VH = 8
SEED = 1
NOISE = 0.0
LEADS = (0.0, 2.0, 3.0, 4.5, 6.0)
PASSES = 25
WAKE = 0.1
NETT = 5.0

DTY = {"aw": ("bfloat16", 2), "af": ("float32", 4), "ai": ("int32", 4), "au": ("uint16", 2), "ah": ("float16", 2)}
_size = {k: 0 for k in DTY}


def new(ar, n):
    a = _size[ar]
    step = 32 // DTY[ar][1]
    _size[ar] = a + (n + step - 1) // step * step
    return (ar, a, a + n, 1)


def sub(h, a, b, s=1):
    return (h[0], h[1] + a, h[1] + b, s)


def ps(bank, slot, n):
    return ("ps%d" % bank, slot * SLOT, slot * SLOT + n, 1)


def ncol(h):
    return (h[2] - h[1] + h[3] - 1) // h[3]


def wide(h):
    return 4 if h[0] not in DTY else DTY[h[0]][1]


def build():
    ops = []
    NB = len(BLOCKS)
    cur = [-1, 0]

    def add(eng, cost, reads, writes, emit, name="", kind="c", sem=None, extra=()):
        ops.append({"e": eng, "c": cost, "r": reads, "w": writes, "f": emit, "n": name, "k": kind, "s": sem, "x": list(extra), "t": cur[0], "blk": cur[1]})
        return len(ops) - 1

    def vts(o, i, s1, s2, op0, op1=None, name="ts"):
        n = ncol(o)
        fast = wide(o) == 2 and wide(i) == 2
        rd = [i] + [s for s in (s1, s2) if isinstance(s, tuple)]

        def f(q, V):
            a = V(s1) if isinstance(s1, tuple) else s1
            if op1 is None:
                return q.tensor_scalar(V(o), V(i), a, None, op0)
            b = V(s2) if isinstance(s2, tuple) else s2
            return q.tensor_scalar(V(o), V(i), a, b, op0, op1)
        return add("V", 0.03 + CY * max(64, n * (0.5 if fast else 1)), rd, [o], f, name)

    def vtt(o, a, b, op, name="tt"):
        n = ncol(o)
        both = a[0] in DTY and b[0] in DTY
        return add("V", 0.03 + CY * max(64, n * (2 if both else 1)), [a, b], [o], lambda q, V: q.tensor_tensor(V(o), V(a), V(b), op), name)

    def vcopy(o, i, name="cp"):
        n = ncol(o)
        fast = wide(o) == 2 and wide(i) == 2
        return add("V", 0.03 + CY * max(64, n * (0.5 if fast else 1)), [i], [o], lambda q, V: q.tensor_copy(V(o), V(i)), name)

    def vset(o, v):
        return add("V", 0.03 + CY * max(64, ncol(o) * (0.5 if wide(o) == 2 else 1)), [], [o], lambda q, V: q.memset(V(o), v), "set")

    def act(o, i, fn, scale=1.0, bias=0.0, acc=None, name="act"):
        def f(q, V):
            if acc is None:
                return q.activation(V(o), V(i), fn, bias, scale)
            return q.activation(V(o), V(i), fn, bias, scale, accum_out=V(acc))
        return add("A", 0.06 + CY * ncol(o), [i], [o] + ([acc] if acc else []), f, name)

    def gath(eng, o, win, off, minus=None, op=None, name="gather"):
        n = ncol(o)
        if eng == "A":
            return add("A", 0.07 + CY * GR * n, [win, off], [o],
                       lambda q, V: q.activation(V(o), V(win).indirect(V(off)), AF.Copy), name)
        if minus is None:
            return add("V", 0.05 + CY * GR * n, [win, off], [o],
                       lambda q, V: q.tensor_copy(V(o), V(win).indirect(V(off))), name)
        return add("V", 0.05 + CY * GR * n, [win, off, minus], [o],
                   lambda q, V: q.tensor_tensor(V(o), V(win).indirect(V(off)), V(minus), op), name)

    def pe(o, terms, name="pe", first=True, stop=True, extra=()):
        c = 0.03
        for l, r in terms:
            c += PEO + PECY * max(64, ncol(r)) * (4 if l[0] == "af" else 1)

        def f(q, V):
            last = None
            for k, (l, r) in enumerate(terms):
                last = q.matmul(V(o), V(l), V(r), first and k == 0, stop and k == len(terms) - 1)
            return last
        return add("P", c, [x for t in terms for x in t], [o], f, name, extra=[i for i in extra if i is not None])

    def mailto(src, land, nm, t, b):
        sem = "%s%d_%d" % (nm, t, b)
        k = add("G", 1.0, [src], [], ("send", src, land, sem), nm, "send")
        add("N", NETT, [], [land], None, nm, "net", sem, (k,))

    X = new("aw", W)
    xin, zin, win_ = X, new("aw", NP), new("aw", 1)
    bain, bbin = new("ai", NP), new("ai", NP)
    for k, (nm, h, q) in enumerate((("ba", bain, "S"), ("bb", bbin, "S"), ("zp", zin, "S"), ("wl", win_, "S"), ("xt", X, "S"))):
        add(q, 0.1, [], [h], lambda q, V, nm=nm, h=h: q.dma_start(V(h), V(nm)), "ld" + nm, "dma", "ld" + nm)

    ONE = new("aw", 128)
    ID, NEG, BO, LT, L64, L4, T1 = [new("aw", 128) for _ in range(7)]
    MID = {v: new("aw", 128) for v in (-64, -2, 4, 2048, -4096, 528384, -2 ** 23, 2 ** 30, 65536, 98304)}
    D, WD = new("aw", 144), new("aw", 144)
    WB, WB64 = new("aw", 128), new("aw", 128)
    HI, H65, H101, H32, HH = [new("ah", 128) for _ in range(5)]
    MONE = new("aw", max(BLOCKS))
    IF = new("af", 128)
    NCM = max(BLOCKS) // 16
    MASK = new("aw", 16 * max(BLOCKS))

    def asel(o, i, pat, cmp, base, cm):
        return add("G", 0.4, [i], [o], lambda q, V: q.affine_select(V(o), V(i), pat, cmp, 0.0, base, cm), "asel")
    vset(ONE, 1.0)
    asel(ID, ONE, [[-1, 128]], OP.is_equal, 0, 1)
    asel(T1, ONE, [[-16, 8], [0, 16]], OP.is_ge, 0, 1)
    asel(BO, T1, [[16, 8], [0, 16]], OP.is_ge, 15, -1)
    asel(LT, BO, [[1, 128]], OP.is_gt, 0, -1)
    B1, B2, BASE = new("ai", NCM), new("ai", NCM), new("ai", NCM)
    add("G", 0.2, [], [B1], lambda q, V: q.iota(V(B1), [[0, NCM]], 0, 16), "iota")
    add("G", 0.2, [], [B2], lambda q, V: q.iota(V(B2), [[256, NCM]], 0, 0), "iota")
    vts(B1, B1, 255, None, OP.bitwise_and)
    vtt(BASE, B1, B2, OP.add)
    vcopy(HI, ID)
    vts(H65, ID, 2080.0, None, OP.mult)
    vts(H101, ID, 3232.0, None, OP.mult)
    vts(H32, ID, 32.0, None, OP.mult)
    vts(NEG, ID, -1.0, None, OP.mult)
    for v in sorted(MID):
        act(MID[v], ID, AF.Copy, scale=float(v))
    act(IF, ID, AF.Copy)
    vtt(L64, LT, MID[-64], OP.add)
    vtt(L4, LT, MID[4], OP.add)
    vset(D, 0.0)
    vcopy(sub(D, 15, 143, 16), sub(BO, 0, 128, 16))
    WF = new("af", 1)
    vcopy(WF, win_)
    vts(WD, D, WF, None, OP.mult)
    vts(WB, BO, WF, None, OP.mult)
    vts(WB64, WB, 2048.0, None, OP.mult)
    vset(MONE, -1.0)
    vts(HH, ID, 0.5, None, OP.mult)
    vset(MASK, 1.0)
    vset(sub(MASK, 0, 16 * max(BLOCKS), 16), 0.0)

    p0 = [sum(BLOCKS[:b]) for b in range(NB)]
    big = []
    for b in range(NB):
        n = BLOCKS[b]
        d = {k: new("aw", 16 * n) for k in ("h", "o", "c", "ch", "ah", "zx", "zs")}
        d.update({k: new("aw", n) for k in ("live", "rec", "want", "am", "sv", "jk", "ry", "ay", "spl", "fl", "so", "fu")})
        d.update({k: new("ah", n) for k in ("Hc", "Oc", "Cc", "tO", "tC", "tH", "s1", "s2")})
        d.update({k: new("af", n) for k in ("dhS", "m", "gl", "dhG", "m2", "stU", "xg", "P", "pU")})
        d.update({k: new("ai", n) for k in ("T", "C", "TU", "xf")})
        d.update({k: new("ai", n // 16) for k in ("ui", "ua", "ul")})
        d["C16"], d["ch16"], d["l16"] = new("au", n), new("au", n), new("au", n // 16)
        vset(d["zs"], 0.0)
        big.append(d)
    ACC = new("af", 16 * NREAD)
    RM = [[new("aw", 128) for _ in range(NB)] for _ in range(2)] * 3
    subn = [0]
    lastv = [None]

    mail = []
    for b in range(NB):
        n = BLOCKS[b]
        A16, B16, I0, G0 = new("au", n), new("au", n), new("aw", n), new("aw", n)
        vcopy(A16, sub(bain, p0[b], p0[b] + n))
        vcopy(B16, sub(bbin, p0[b], p0[b] + n))
        vset(I0, 0.0)
        vset(G0, 0.0)
        mail.append((A16, B16, sub(zin, p0[b], p0[b] + n), I0, G0))

    for t in range(NREAD):
        last = t == NREAD - 1
        nxt = []
        for b in range(NB):
            cur[0], cur[1] = t, b
            n, d, par = BLOCKS[b], big[b], b & 1
            H16, O16, z, I, G = mail[b][t & 1], mail[b][1 - (t & 1)], mail[b][2], mail[b][3], mail[b][4]
            hp, lin = ps(2, 2 * par, n), ps(2, 2 * par + 1, n)
            sg = ps(3 + par, 3, n)
            vts(d["Hc"], H16, -2048.0, None, OP.add, name="Hc")
            vts(d["Oc"], O16, -2048.0, None, OP.add, name="Oc")
            pe(hp, [(HI, d["Hc"])], "HcPS")
            pe(lin, [(H65, d["Hc"]), (H101, d["Oc"])], "lin")
            vtt(d["P"], d["Oc"], hp, OP.mult, "P")
            vtt(d["T"], d["P"], lin, OP.add, "T")
            vts(d["C"], d["T"], 5, 4095, OP.arith_shift_right, OP.bitwise_and, name="C")
            vcopy(d["C16"], d["C"], "C16")
            vts(d["Cc"], d["C16"], -2048.0, None, OP.add, name="Cc")
            vtt(d["live"], d["Oc"], hp, OP.not_equal, "live")
            act(sub(d["zs"], 0, 16 * n, 16), z, AF.Copy, name="zs")
            mk = sub(MASK, 0, 16 * n)
            add("V", 0.03 + CY * 8 * n, [mk, d["zs"]], [d["zx"]],
                lambda q, V, mk=mk, d=d: q.tensor_tensor_scan(V(d["zx"]), V(mk), V(d["zs"]), 0.0, OP.mult, OP.add), "zx")
            act(sg, G, AF.Sign, scale=-1.0, bias=1.5, name="sg")
            vtt(d["gl"], d["live"], sg, OP.mult, "gl")
        for b in range(NB):
            cur[0], cur[1] = t, b
            n, d, par = BLOCKS[b], big[b], b & 1
            H16, O16, z, I, G = mail[b][t & 1], mail[b][1 - (t & 1)], mail[b][2], mail[b][3], mail[b][4]
            dh, do, dc, cap = [ps(3 + par, k, n) for k in range(4)]
            vs = ps(5, b, n)
            pc = [(k * n // PIECES, (k + 1) * n // PIECES) for k in range(PIECES)]
            for k, lst, dist in (("h", H16, dh), ("o", O16, do), ("c", d["C16"], dc)):
                res = d["ah"] if k == "h" else d[k]
                for (q0, q1), mode in zip(pc, MODE[b][k]):
                    e0, e1 = 16 * q0, 16 * q1
                    if mode == "F":
                        gath("V", sub(d[k], e0, e1), X, sub(lst, q0, q1), sub(d["zx"], e0, e1), OP.subtract, k)
                        act(sub(res, e0, e1), sub(d[k], e0, e1), AF.Abs, name="abs" + k)
                        continue
                    gath(mode, sub(d[k], e0, e1), X, sub(lst, q0, q1), name=k)
                    for a0 in range(e0, e1, 512):
                        a1 = min(a0 + 512, e1)
                        tile = ("ps%d" % (subn[0] & 1), 0, a1 - a0, 1)
                        subn[0] += 1
                        pe(tile, [(ID, sub(d[k], a0, a1)), (NEG, sub(d["zx"], a0, a1))], "sub")
                        act(sub(res, a0, a1), tile, AF.Abs, name="abs" + k)
                for q0, q1 in (pc if k in SPLIT else [(0, n)]):
                    pe(sub(dist, q0, q1), [(sub(D, 15 - j, 143 - j), sub(res, 16 * q0 + j, 16 * q1, 16)) for j in range(16)], "d" + k)
                if k == "h":
                    for j0 in range(0, 16, VH):
                        terms = [(NEG, sub(d["h"], j, 16 * n, 16)) for j in range(j0, j0 + VH)]
                        pe(vs, terms, "voteh", first=j0 == 0, stop=False, extra=lastv)
            act(d["dhS"], dh, AF.Copy, name="dhS")
            vtt(d["dhG"], d["gl"], dh, OP.mult, "dhG")
            vtt(d["m2"], d["dhG"], do, OP.min, "m2")
            vtt(d["m"], d["dhS"], dc, OP.min, "m")
            vtt(d["want"], d["m2"], dc, OP.is_gt, "want")
            vtt(d["rec"], d["m"], do, OP.is_ge, "rec")
            pe(cap, [(L64, d["want"])], "cap")
            vts(d["am"], cap, -60.0, None, OP.is_lt, name="am")
            rp, ap_, sp_, cs = dh, do, dc, cap
            pe(rp, [(ID, d["rec"])], "recPS")
            vtt(d["tO"], d["Oc"], rp, OP.mult, "tO")
            pe(ap_, [(ID, d["am"])], "amPS")
            pe(sp_, [(ID, sub(ONE, 0, n)), (NEG, d["rec"]), (NEG, d["am"])], "sH")
            vtt(d["tC"], d["Cc"], ap_, OP.mult, "tC")
            vtt(d["tH"], d["Hc"], sp_, OP.mult, "tH")
            pe(cs, [(HI, d["tO"]), (HI, d["tC"]), (HI, d["tH"])], "chS")
            vts(d["ch16"], cs, 2048.0, None, OP.add, name="ch16")
            for (q0, q1), e in zip(pc, CHQ[b]):
                gath(e, sub(d["ch"], 16 * q0, 16 * q1), X, sub(d["ch16"], q0, q1), name="ch")
            lastv[0] = pe(vs, [(ID, sub(d["ch"], j, 16 * n, 16)) for j in range(16)], "vote", first=False)
        for b in range(NB):
            cur[0], cur[1] = t, b
            n, d, par = BLOCKS[b], big[b], b & 1
            z = mail[b][2]
            mx = d["zx"]
            for k in range(PIECES):
                q0, q1 = 16 * (k * n // PIECES), 16 * ((k + 1) * n // PIECES)
                mk, cp, mp = sub(MASK, 0, q1 - q0), sub(d["ch"], q0, q1), sub(mx, q0, q1)
                add("V", VO + CY * (q1 - q0) / 2, [mk, cp], [mp],
                    lambda q, V, mk=mk, cp=cp, mp=mp: q.tensor_tensor_scan(V(mp), V(mk), V(cp), 0.0, OP.mult, OP.max), "mx")
            M = sub(mx, 15, 16 * n, 16)
            ur, uc = ps(6, 2 * par, n), ps(6, 2 * par + 1, n)
            d["M"], d["ur"], d["uc"] = M, ur, uc
            out = {}
            if not last:
                out["AB"] = new("au", 2 * n)
                out["ZIG"] = new("aw", 3 * n)
                out["A"], out["B"] = sub(out["AB"], 0, n), sub(out["AB"], n, 2 * n)
                out["z"], out["I"], out["G"] = [sub(out["ZIG"], k * n, (k + 1) * n) for k in range(3)]
                ulp = sub(uc, 0, n // 16)
                pe(ulp, [(sub(WD, 15 - j, 143 - j), sub(mx, 15 + 16 * j, 16 * n, 256)) for j in range(16)], "ulist")
                vcopy(d["ui"], ulp, "ui")
                vts(d["ua"], d["ui"], 15, None, OP.bitwise_and, name="ua")
                vtt(d["ul"], d["ua"], sub(BASE, 0, n // 16), OP.add, "ul")
                vcopy(d["l16"], d["ul"], "l16")
                xw = sub(X, 16 * p0[b], 16 * (p0[b] + n))
                gath("V", d["xg"], xw, d["l16"], M, OP.add, "xg")
                vts(d["xf"], d["xg"], -0.5, 0.5, OP.add, OP.mult, name="xf")
                add("V", 0.05 + CY * 3.8 * n, [d["xf"], d["l16"]], [xw],
                    lambda q, V, d=d, xw=xw: q.tensor_copy(V(xw).indirect(V(d["l16"])), V(d["xf"])), "scat")
            else:
                out["A"], out["B"], out["I"], out["G"] = [new("af", n) for _ in range(4)]
            d["out"] = out
        for b in range(NB):
            cur[0], cur[1] = t, b
            n, d, par = BLOCKS[b], big[b], b & 1
            H16, O16, z, I, G = mail[b][t & 1], mail[b][1 - (t & 1)], mail[b][2], mail[b][3], mail[b][4]
            out, M, ur, uc = d["out"], d["M"], d["ur"], d["uc"]
            one = sub(ONE, 0, n)
            S0, S1, S2, S3 = [ps(3 + par, k, n) for k in range(4)]
            vs, cn = ps(5, b, n), S3
            old0, old1 = ps(2, 2 * par, n), ps(2, 2 * par + 1, n)
            yes, nm = ps(7, 2 * par, n), ps(7, 2 * par + 1, n)
            act(d["sv"], vs, AF.Sign, bias=0.5, name="sv")
            pe(cn, [(BO, d["sv"])], "cnt")
            acc = sub(ACC, 16 * t + b, 16 * t + b + 1)
            act(yes, cn, AF.Sign, bias=0.5, acc=None if last else acc, name="yes")
            if not last:
                rm = RM[t][b]
                add("A", 0.06 + CY * 128, [ONE, acc], [rm], lambda q, V, rm=rm, acc=acc: q.activation(V(rm), V(ONE), AF.Copy, 0.0, V(acc)), "RM")
                pe(old1, [(ID, z), (NEG, M)], "zd")
                act(out["z"], old1, AF.Abs, name="z")
            vtt(d["ry"], d["rec"], yes, OP.is_equal, "ry")
            vtt(d["ay"], d["am"], yes, OP.is_equal, "ay")
            pe(old0, [(ID, G), (ID, d["ay"])], "Gs")
            act(out["G"], old0, AF.Copy, name="G")
            pe(S0, [(ID, d["ry"]), (ID, d["ay"])], "mv")
            vtt(nm, d["live"], S0, OP.is_gt, "nm")
            vtt(out["I"], I, nm, OP.not_equal, "I")
            vtt(d["spl"], I, nm, OP.mult, "spl")
            if not last:
                zl, lh, lo = new("aw", 3 * n), new("au", n), new("au", n)
                mailto(out["ZIG"], zl, "rz", t, b)
            pe(S1, [(LT, d["spl"])], "bef")
            act(d["fl"], S1, AF.Copy, scale=0.5, bias=128.75, name="fl")
            pe(S2, [(L4, d["spl"]), (MID[-2], d["fl"])], "par")
            vts(d["so"], S2, -253.5, None, OP.is_gt, name="so")
            pe(S3, [(ID, one), (NEG, d["ry"]), (NEG, d["ay"]), (NEG, d["so"])], "sH2")
            pe(S0, [(ID, d["ay"]), (ID, d["so"])], "a2")
            vtt(d["s1"], d["tO"], yes, OP.mult, "tO2")
            vtt(d["tC"], d["Cc"], S0, OP.mult, "tC2")
            vtt(d["tH"], d["Hc"], S3, OP.mult, "tH2")
            pe(S1, [(HH, d["tO"]), (HH, d["s1"]), (HI, d["tC"]), (HI, d["tH"])], "nHs")
            oh, oo = (out["A"], out["B"]) if t % 2 == 0 else (out["B"], out["A"])
            vts(oh, S1, 2048.0, None, OP.add, name="nH")
            if not last:
                mailto(oh, lh, "rh", t, b)
            pe(ur, [(WB, M)], "uraw")
            act(d["fu"], ur, AF.Copy, scale=1.0 / 4096, bias=128.5 + 1.0 / 8192, name="fu")
            pe(uc, [(MID[528384], one), (MID[-4096], d["fu"]), (WB, M)], "u")
            lin = [(WB64, M), (MID[-2 ** 23], d["fu"]), (MID[2 ** 30], one), (H32, d["Hc"]), (MID[98304 if t else 65536], one)]
            if t > 0:
                lin += [(RM[t - 1][k], sub(MONE, 0, n)) for k in range(NB)]
            vtt(d["pU"], d["Hc"], uc, OP.mult, "pU")
            pe(ur, lin, "linU")
            vtt(d["TU"], d["pU"], ur, OP.add, "TU")
            vts(d["TU"], d["TU"], 5, 4095, OP.arith_shift_right, OP.bitwise_and, name="U")
            pe(S3, [(ID, d["live"]), (NEG, d["spl"])], "sO")
            pe(S0, [(ID, one), (NEG, d["live"])], "st")
            vtt(d["stU"], d["TU"], S0, OP.mult, "stU")
            vtt(d["s2"], d["Oc"], S3, OP.mult, "s2")
            vtt(d["s1"], d["spl"], S1, OP.mult, "s1")
            pe(S2, [(MID[2048], d["live"]), (IF, d["stU"]), (HI, d["s2"]), (HI, d["s1"])], "nOs")
            vcopy(oo, S2, "nO")
            if not last:
                mailto(oo, lo, "ro", t, b)
                nxt.append(((lh, lo) if t % 2 == 0 else (lo, lh)) + (sub(zl, 0, n), sub(zl, n, 2 * n), sub(zl, 2 * n, 3 * n)))
            else:
                for k, nme in (("G", "yg"), ("I", "yi"), ("A", "ya"), ("B", "yb")):
                    add("S", 0.1, [out[k]], [], lambda q, V, nme=nme, h=out[k], a=p0[b], n=n: q.dma_start(V(nme)[:, a:a + n], V(h)), "st" + nme, "dma", "st%s%d" % (nme, b))
        mail = nxt
    return ops


def depend(ops):
    hist = {}
    for i, o in enumerate(ops):
        dep = set(o["x"])
        for h, w in [(h, 0) for h in o["r"]] + [(h, 1) for h in o["w"]]:
            for j, a, b, jw in hist.get(h[0], ()):
                if (w or jw) and a < h[2] and h[1] < b:
                    dep.add(j)
        for h, w in [(h, 0) for h in o["r"]] + [(h, 1) for h in o["w"]]:
            lst = hist.setdefault(h[0], [])
            if w:
                lst[:] = [e for e in lst if not (h[1] <= e[1] and e[2] <= h[2] and h[3] == 1)]
            lst.append((i, h[1], h[2], w))
        dep.discard(i)
        o["d"] = sorted(dep)
        o["b"] = sorted({h[0] for h in o["r"] + o["w"] if h[0] not in DTY})


LDT = {"ldba": 3.0, "ldbb": 3.2, "ldzp": 3.4, "ldwl": 3.4, "ldxt": 7.0}


def schedule(ops, pri, pred, succ):
    n = len(ops)
    left = [len(p) for p in pred]
    ready = {}
    est = [0.0] * n
    free, bank = {}, {}
    end, start = [0.0] * n, [0.0] * n
    for i in range(n):
        if not left[i]:
            ready.setdefault(ops[i]["e"], []).append(i)
    order, done = [], 0
    while done < n:
        best = None
        for e, lst in ready.items():
            if not lst:
                continue
            t0 = free.get(e, 0.0) if e != "N" else 0.0
            cand = []
            for i in lst:
                s = max(t0, est[i])
                for b in ops[i]["b"]:
                    for e2, u in bank.get(b, {}).items():
                        if e2 != e:
                            s = max(s, u + WAKE)
                cand.append((s, -pri[i], i))
            s0 = min(cand)[0]
            c = min((c for c in cand if c[0] <= s0 + WIN), key=lambda c: c[1])
            if best is None or c[0] < best[0]:
                best = (c[0], c[2], e)
        s, i, e = best
        ready[e].remove(i)
        o = ops[i]
        start[i] = s
        end[i] = s + o["c"]
        fin = end[i]
        if o["k"] == "dma":
            fin = s + LDT.get(o["n"], 2.5)
        free[e] = end[i]
        for b in o["b"]:
            bank.setdefault(b, {})[e] = end[i]
        order.append(i)
        done += 1
        for j in succ[i]:
            est[j] = max(est[j], fin + (WAKE if ops[j]["e"] != e else 0.06))
            left[j] -= 1
            if not left[j]:
                ready.setdefault(ops[j]["e"], []).append(j)
        end[i] = fin
    return order, start, end


def plan(ops):
    n = len(ops)
    pred = [o["d"] for o in ops]
    succ = [[] for _ in ops]
    for i in range(n):
        for j in pred[i]:
            succ[j].append(i)
    path = [0.0] * n
    for i in range(n - 1, -1, -1):
        path[i] = ops[i]["c"] + max([path[j] + WAKE for j in succ[i]], default=0.0)
    best = None
    seed = [SEED]

    def rnd():
        seed[0] = (seed[0] * 1103515245 + 12345) % 2147483648
        return seed[0] / 1073741824.0 - 1.0

    for lead in LEADS:
        pri = [p + (lead if o["t"] >= 0 and o["blk"] == 0 else 0.0) for p, o in zip(path, ops)]
        for _ in range(PASSES):
            order, start, end = schedule(ops, pri, pred, succ)
            if best is None or max(end) < max(best[2]):
                best = (order, start, end)
            back = schedule(ops, end, succ, pred)[2]
            pri = [x + NOISE * rnd() for x in back]
    return best


OPS = build()
depend(OPS)
ORDER, START, END = plan(OPS)

SCRATCH = {k: ("sbuf", [128, _size[k]], DTY[k][0]) for k in DTY}
SCRATCH.update({"ps%d" % k: ("psum", [128, 512], "float32") for k in range(8)})
SEMAPHORES = ["cV", "cA", "cP", "cG", "sent"] + sorted({o["s"] for o in OPS if o["s"]})


def rank_program(g, core, T, topo):
    rank = T.rank_of(core)
    if rank is None:
        return
    dst = T.cores[(rank + 1) % len(T.cores)]
    rid, pid, _ = topo.addr(dst)
    mask = topo.mask(core, dst)
    width = len(topo.engines(core, dst))
    queue = {"V": g.vector, "A": g.scalar, "P": g.tensor, "G": g, "S": g.sync}

    def V(h):
        if isinstance(h, str):
            return T[h][:]
        if h[3] == 1:
            return T[h[0]][:, h[1]:h[2]]
        return T[h[0]][:, h[1]:h[2]:h[3]]

    count = {e: 0 for e in "VAPG"}
    know = {e: {} for e in queue}
    snap = {}
    lastb = {}
    sent = 0
    sig = {}

    def need(e, i):
        s, c = sig[i]
        if know[e].get(s, 0) >= c:
            return
        queue[e].wait_ge(T.sem[s], c)
        for k, v in snap[i].items():
            if know[e].get(k, 0) < v:
                know[e][k] = v
        know[e][s] = c

    for i in ORDER:
        o = OPS[i]
        e = o["e"]
        if o["k"] == "net":
            sig[i] = (o["s"], width)
            snap[i] = {}
            continue
        deps = {j for j in o["d"] if OPS[j]["k"] != "send"}
        for b in o["b"]:
            for e2, j in lastb.get(b, {}).items():
                if e2 != e:
                    deps.add(j)
        for j in sorted(deps, key=lambda j: -START[j]):
            need(e, j)
        if o["k"] == "send":
            _s, src, land, sem = o["f"]
            g.remote_dma(V(land), V(src), T.sem[sem], T.sem.sent, pid, rid, mask)
            sent += width
            continue
        ins = o["f"](queue[e], V)
        if o["k"] == "dma":
            ins.then_inc(T.sem[o["s"]], 16)
            sig[i] = (o["s"], 16)
            snap[i] = dict(know[e])
        else:
            count[e] += 1
            ins.then_inc(T.sem["c" + e], 1)
            sig[i] = ("c" + e, count[e])
            snap[i] = dict(know[e])
            for b in o["b"]:
                lastb.setdefault(b, {})[e] = i
    for e in "VAPG":
        g.wait_ge(T.sem["c" + e], count[e])
    for i in ORDER:
        if OPS[i]["k"] in ("dma", "net"):
            g.wait_ge(T.sem[OPS[i]["s"]], sig[i][1])
    g.wait_ge(T.sem.sent, sent)
